import numpy as np
import ml_dtypes


def mxq(x, axis, fmt="e4m3"):
    dtype, down = {"e4m3": (ml_dtypes.float8_e4m3fn, 7), "e5m2": (ml_dtypes.float8_e5m2, 14)}[fmt]
    v = np.moveaxis(np.asarray(x, np.float32).astype(ml_dtypes.bfloat16).astype(np.float64), axis, -1)
    blocks = v.reshape(v.shape[:-1] + (-1, 32))
    amax = np.abs(blocks).max(-1, keepdims=True)
    byte = np.maximum(np.where(amax > 0, np.frexp(amax)[1] - 1 + 127, 0) - down, 1)
    scale = np.exp2(byte - 127.0)
    codes = (blocks / scale).astype(np.float32).astype(dtype).astype(np.float64)
    return np.moveaxis((codes * scale).reshape(v.shape), -1, axis)


WIDE = False


def mx_kscale(k):
    if not WIDE:
        return np.ones(k)
    levels = np.array([10, -10, 5, -5, 0])
    if k % 512:
        return np.exp2(np.random.permutation(np.resize(levels, k // 32))).repeat(32)
    a = np.empty((k // 512, 16))
    for p in range(k // 512):
        a[p, :8] = np.random.permutation(np.resize(levels, 8))
        for g in range(8):
            far = levels[np.abs(levels - a[p, g]) >= 10]
            a[p, g + 8] = far[np.random.randint(len(far))]
    return np.exp2(a.ravel()).repeat(32)


BF16 = ml_dtypes.bfloat16


def bf(x):
    return np.asarray(x, np.float32).astype(BF16)


def f64(x):
    return np.asarray(x).astype(np.float64)


B, D, H, C = 4096, 1024, 1024, 128


def draw0():
    s, t = mx_kscale(D), mx_kscale(H)
    return {
        "x": bf(np.random.standard_normal((B, D)) * s),
        "w1": bf(np.random.standard_normal((D, H)) * 1.2 / np.sqrt(D) / s[:, None]),
        "g1": bf((1.0 + 0.1 * np.random.standard_normal(H)) * t),
        "v1": bf(np.random.standard_normal((H, C)) / np.sqrt(H) / t[:, None]),
        "wx": bf(np.random.standard_normal((D, C)) * 0.8 / np.sqrt(D) / s[:, None]),
        "wh": bf(np.random.standard_normal((H, C)) * 1.2 / np.sqrt(H) / t[:, None]),
        "u": bf(np.random.standard_normal((B, C))),
    }


def centred_features(xq, w1, g1):
    r = np.maximum(xq @ mxq(f64(w1), 0, "e4m3"), 0.0)
    return (r - np.mean(r, axis=0, keepdims=True)) * f64(g1)[None, :]


def newton_target(y, score):
    return y * (1.0 + np.exp(-y * score))


def core(x, w1, g1, v1, wx, wh, u):
    xq = mxq(f64(x), 1, "e4m3")
    h = centred_features(xq, w1, g1)
    hq = mxq(h, 1, "e4m3")
    s1 = hq @ mxq(f64(v1), 0, "e4m3")
    p = (xq @ mxq(f64(wx), 0, "e4m3")) + (hq @ mxq(f64(wh), 0, "e4m3"))
    score = 0.8 * s1 + 0.8 * np.tanh(p)
    y = np.where(f64(u) < 0, -1.0, 1.0)
    return newton_target(y, score)


def e4m3fn_bytes(y):
    return np.clip(np.asarray(y, np.float64), -448.0, 448.0).astype(np.float32).astype(ml_dtypes.float8_e4m3fn).view(np.uint8)


def e4m3fn_values(b):
    return np.asarray(b, np.uint8).view(ml_dtypes.float8_e4m3fn).astype(np.float64)


def setup_inputs():
    d = draw0()
    x0 = np.asarray(d['x']).astype(np.float64)
    s = (np.max(np.abs(x0), axis=(0,), keepdims=True) / 448.0).astype(np.float32)
    out = {}
    for k, v in d.items():
        if k == 'x':
            out['x_bytes'] = e4m3fn_bytes(x0 / s.astype(np.float64))
            out['x_scale'] = s
        else:
            out[k] = v
    return out


def reference(x_bytes, x_scale, w1, g1, v1, wx, wh, u):
    return core(e4m3fn_values(x_bytes) * x_scale.astype(np.float64), w1, g1, v1, wx, wh, u)

from contextlib import ExitStack

import concourse.mybir as mybir
from concourse.masks import make_identity

B, D, H, C = 4096, 1024, 1024, 128
FLOPS = 2 * B * D * H + 3 * 2 * B * D * C

F32 = mybir.dt.float32
BF16 = mybir.dt.bfloat16
U32 = mybir.dt.uint32
U8 = mybir.dt.uint8
F8 = mybir.dt.float8_e4m3fn
X4 = mybir.dt.float8_e4m3fn_x4
ACT = mybir.ActivationFunctionType
ALU = mybir.AluOpType
AX = mybir.AxisListType

P = 128
NC = 512
CH = B // NC
RT = NC // P
KP = D // 512
LN2 = 0.6931471805599453


def tile_grownetnewtontargets_t_kernel(tc, x_bytes, x_scale, w1, g1, v1, wx, wh, u, out):
    nc = tc.nc
    x_view = x_bytes.rearrange("(p j) k -> p j k", p=P)
    u_view = u.rearrange("(p j) c -> p j c", p=P)
    out_view = out.rearrange("(p j) c -> p j c", p=P)
    w1_view = w1.rearrange("(g p j) h -> g p j h", p=P, j=4)

    with ExitStack() as ctx:
        keep = ctx.enter_context(tc.tile_pool(name="keep", bufs=1))
        rpool = ctx.enter_context(tc.tile_pool(name="rpool", bufs=40))
        psum = ctx.enter_context(tc.psum_pool(name="psum", bufs=4))

        scale_bc = keep.tile([P, D], F32, name="scale_bc")
        nc.scalar.dma_start(out=scale_bc[:], in_=x_scale.rearrange("o k -> (o k)").partition_broadcast(P))
        g_bf = keep.tile([P, 8], BF16, name="g_bf")
        g_f32 = keep.tile([P, 8], F32, name="g_f32")
        sums = keep.tile([P, 8, CH], F32, name="sums")
        mean = keep.tile([P, 8], F32, name="mean")
        warm = keep.tile([P, 1], F32, name="warm")
        ident = keep.tile([P, P], F32, name="ident")
        nc.vector.memset(warm[:], 0.0)
        nc.scalar.activation(out=warm[:], in_=warm[:], func=ACT.Exp)
        make_identity(nc, ident[:])

        xq, xqs = [], []
        for c in range(CH):
            q = keep.tile([P, KP, NC], U32, name=f"xq{c}", align_bytes=64)
            qs = keep.tile([P, KP, NC], U8, name=f"xqs{c}", align_bytes=64)
            xq.append(q)
            xqs.append(qs)
        w1q, w1s = {}, {}
        for a in range(2):
            for g in range(KP):
                wq = keep.tile([P, 512], U32, name=f"w1q{a}{g}", align_bytes=64)
                ws = keep.tile([P, 512], U8, name=f"w1s{a}{g}", align_bytes=64)
                w1q[a, g] = wq
                w1s[a, g] = ws
        small = {}
        for n in ("v1", "wx", "wh"):
            sq = keep.tile([P, KP, C], U32, name=f"{n}q", align_bytes=64)
            ss = keep.tile([P, KP, C], U8, name=f"{n}s", align_bytes=64)
            small[n] = (sq, ss)

        raw, inter = {}, {}
        u_sb = keep.tile([P, B // P, C], BF16, name="u_sb")
        y2 = u_sb
        for n in ("v1", "wx", "wh"):
            rw = keep.tile([P, KP, 4, C], BF16, name=f"{n}raw")
            raw[n] = rw

        def small_copy(n):
            it = keep.tile([P, KP * C * 4], BF16, tag="smallint", align_bytes=64)
            nc.vector.tensor_copy(out=it[:].rearrange("p (g c j) -> p g c j", g=KP, j=4),
                                  in_=raw[n][:].rearrange("p g j c -> p g c j"))
            inter[n] = it

        def small_quant(n):
            sq, ss = small[n]
            nc.vector.quantize_mx(out=sq[:].rearrange("p g c -> p (g c)").bitcast(X4),
                                  scales=ss[:].rearrange("p g c -> p (g c)"), in_=inter[n][:])

        def means(a, t0, t1):
            i0, i1 = 4 * a + t0, 4 * a + t1
            nc.vector.reduce_sum(out=mean[:, i0:i1], in_=sums[:, i0:i1, :], axis=AX.X)
            nc.vector.tensor_scalar(out=mean[:, i0:i1], in0=mean[:, i0:i1], scalar1=1.0 / B, scalar2=None, op0=ALU.mult)

        r = {}

        def stage1(a, t, c):
            z = psum.tile([P, NC], F32, tag="z")
            for g in range(KP):
                nc.tensor.matmul_mx(
                    out=z[:],
                    lhsT=w1q[a, g][:, P * t:P * t + P].bitcast(X4),
                    lhsT_scale=w1s[a, g][:, P * t:P * t + P],
                    rhs=xq[c][:, g, :].bitcast(X4),
                    rhs_scale=xqs[c][:, g, :],
                    start=(g == 0),
                    stop=(g == KP - 1),
                )
            return z

        def evac(z, a, t, c):
            rt = rpool.tile([P, NC], F32, tag="r")
            nc.scalar.activation(out=rt[:], in_=z[:], func=ACT.Relu,
                                 accum_out=sums[:, 4 * a + t, c:c + 1])
            r[a, t, c] = rt

        with ExitStack() as actx:
            xraw_pool = actx.enter_context(tc.tile_pool(name="xraw_pool", bufs=3))
            xs_pool = actx.enter_context(tc.tile_pool(name="xs_pool", bufs=4))
            grp_pool = actx.enter_context(tc.tile_pool(name="grp_pool", bufs=2))
            w_pool = actx.enter_context(tc.tile_pool(name="w_pool", bufs=2))

            xraw, xs, xt, grp, wraw, wint = {}, {}, {}, {}, {}, {}

            def load_x(c):
                xr = xraw_pool.tile([P, RT, D], U8, tag="xr")
                nc.sync.dma_start(out=xr[:], in_=x_view[:, RT * c:RT * c + RT, :])
                xraw[c] = xr

            def load_w(a, g):
                wr = w_pool.tile([P, 4, 512], BF16, tag="wr")
                nc.sync.dma_start(out=wr[:], in_=w1_view[g][:, :, 512 * a:512 * a + 512])
                wraw[a, g] = wr

            def mult(c, j):
                xm = xs_pool.tile([P, D], BF16, tag="xm")
                nc.vector.tensor_tensor(out=xm[:], in0=xraw[c][:, j, :].bitcast(F8), in1=scale_bc[:], op=ALU.mult)
                xs[c, j] = xm

            def turn(c, j):
                tt = psum.tile([P, 512], F32, tag="side")
                words = xs[c, j][:].bitcast(F32)
                for g in range(KP):
                    for v in range(2):
                        i = 2 * g + v
                        nc.tensor.transpose(tt[:, P * i:P * i + P], words[:, 256 * g + v:256 * (g + 1):2], ident[:])
                xt[c, j] = tt

            def copy_out(c, j):
                if j == 0:
                    gr = grp_pool.tile([P, KP * NC * 4], BF16, tag="gr", align_bytes=64)
                    grp[c] = gr
                dst = grp[c][:].bitcast(F32).rearrange("p (g n v) -> p g n v", g=KP, v=2)
                nc.scalar.copy(out=dst[:, :, P * j:P * j + P, :],
                               in_=xt[c, j][:].rearrange("p (g v n) -> p g n v", g=KP, v=2))

            def quant_x(c):
                for g in range(KP):
                    nc.vector.quantize_mx(out=xq[c][:, g, :].bitcast(X4), scales=xqs[c][:, g, :],
                                          in_=grp[c][:, 4 * NC * g:4 * NC * (g + 1)])

            def w_piece(a, g, t):
                if t == 0:
                    wi = w_pool.tile([P, 2048], BF16, tag="wi", align_bytes=64)
                    wint[a, g] = wi
                dst = wint[a, g][:].rearrange("p (t m j) -> p t m j", t=4, j=4)
                src = wraw[a, g][:].rearrange("p j (m t) -> p t m j", t=4)
                nc.scalar.copy(out=dst[:, t, :, :], in_=src[:, t, :, :])

            def quant_w(a, g):
                nc.vector.quantize_mx(out=w1q[a, g][:].bitcast(X4), scales=w1s[a, g][:], in_=wint[a, g][:])

            load_x(0)
            load_w(0, 0)
            load_w(0, 1)
            load_x(1)
            load_x(2)
            nc.sync.dma_start(out=g_bf[:].rearrange("p (a t) -> p a t", t=4), in_=g1.rearrange("(a p t) -> p a t", p=P, t=4))
            load_w(1, 0)
            load_w(1, 1)
            for c in range(3, CH):
                load_x(c)
            for n, ap in (("v1", v1), ("wx", wx), ("wh", wh)):
                nc.sync.dma_start(out=raw[n][:], in_=ap.rearrange("(g p j) c -> p g j c", p=P, j=4))
            nc.sync.dma_start(out=u_sb[:], in_=u_view)

            pieces_b = [(1, g, t) for g in range(KP) for t in range(4)]

            def prepare(c, j):
                mult(c, j)
                turn(c, j)
                copy_out(c, j)

            def features_a(c):
                for t in range(4):
                    z = stage1(0, t, c)
                    evac(z, 0, t, c)

            for j in range(RT):
                prepare(0, j)
            for g in range(KP):
                for t in range(4):
                    w_piece(0, g, t)
            for j in range(RT):
                prepare(1, j)
            quant_w(0, 0)
            quant_w(0, 1)
            quant_x(0)
            features_a(0)
            nc.vector.tensor_copy(out=g_f32[:], in_=g_bf[:])
            for s in range(2, CH + 1):
                if s < CH:
                    prepare(s, 0)
                    prepare(s, 1)
                quant_x(s - 1)
                features_a(s - 1)
                if s < CH:
                    prepare(s, 2)
                    prepare(s, 3)
                    w_piece(*pieces_b.pop(0))
                    if s == 3 or s == 5:
                        w_piece(*pieces_b.pop(0))
                    if s == 5:
                        quant_w(1, 0)
                    if s == 7:
                        quant_w(1, 1)
            for n in ("v1", "wx", "wh"):
                small_copy(n)
                small_quant(n)
            nc.vector.tensor_scalar(out=y2[:], in0=u_sb[:], scalar1=0.0, scalar2=0.5, op0=ALU.is_ge, op1=ALU.subtract)

        hpool = ctx.enter_context(tc.tile_pool(name="hpool", bufs=2))
        epool = ctx.enter_context(tc.tile_pool(name="epool", bufs=2))
        hkeep = ctx.enter_context(tc.tile_pool(name="hkeep", bufs=1))

        hp, hi, hq, hqs = {}, {}, {}, {}

        split = {}

        def centre(a, c, t, flat=False):
            if (a, c) not in hp:
                if a == 0:
                    pr = hpool.tile([P, 2, NC, 2], BF16, tag="pra")
                else:
                    pr = hpool.tile([P, 2, NC, 2], BF16, tag="prb", bufs=6)
                hp[a, c] = pr
                split[a, c] = flat
            i = 4 * a + t
            dst = hp[a, c][:, t // 2, :, t % 2]
            if split[a, c]:
                dst = hp[a, c][:].rearrange("p v n e -> p (v n e)")[:, NC * t:NC * t + NC]
            nc.vector.tensor_scalar(out=dst, in0=r[a, t, c][:],
                                    scalar1=mean[:, i:i + 1], scalar2=g_f32[:, i:i + 1],
                                    op0=ALU.subtract, op1=ALU.mult)

        def words(a, c):
            it = hpool.tile([P, NC * 4], BF16, tag="it", align_bytes=64)
            flat = hp[a, c][:].rearrange("p v n e -> p (v n e)")
            if split[a, c]:
                nc.scalar.copy(out=it[:].rearrange("p (n t) -> p n t", t=4), in_=flat.rearrange("p (t n) -> p n t", t=4))
            else:
                nc.scalar.copy(out=it[:].bitcast(F32).rearrange("p (n v) -> p n v", v=2),
                               in_=flat.bitcast(F32).rearrange("p (v n) -> p n v", v=2))
            hi[a, c] = it

        def quant_h(a, c):
            if a == 0:
                q = hkeep.tile([P, NC], U32, name=f"hq{c}", align_bytes=64)
                qs = hkeep.tile([P, NC], U8, name=f"hqs{c}", align_bytes=64)
            else:
                q = hpool.tile([P, NC], U32, tag="hq", align_bytes=64)
                qs = hpool.tile([P, NC], U8, tag="hqs", align_bytes=64)
            nc.vector.quantize_mx(out=q[:].bitcast(X4), scales=qs[:], in_=hi[a, c][:])
            hq[a, c] = q
            hqs[a, c] = qs

        means(0, 0, 4)
        order = [(t, c) for t in range(4) for c in range(CH)]
        early = [(0, 0), (0, 1), (0, 2), (0, 3), (1, 0), (1, 1), (1, 2), (1, 3), (2, 0), (2, 1), (2, 2), (2, 3), (0, 4), (1, 4)]
        done = set()
        for s in range(CH + 1):
            if s < CH:
                for t in range(4):
                    centre(0, s, t)
                for t, c in order[4 * s:4 * s + 4]:
                    z = stage1(1, t, c)
                    evac(z, 1, t, c)
                words(0, s)
            if s in (2, 4, 6):
                means(1, s // 2 - 1, s // 2)
            if s >= 2:
                for k in range(2):
                    t, c = early.pop(0)
                    centre(1, c, t)
                    done.add((t, c))
            if s >= 1:
                quant_h(0, s - 1)
        means(1, 3, 4)

        pp, ps, sc = {}, {}, {}

        def stage2(c):
            pt = psum.tile([P, RT, C], F32, tag="side")
            st = psum.tile([P, RT, C], F32, tag="side")
            for i in range(RT):
                cols = slice(P * i, P * i + P)
                steps = [(xq[c][:, g, cols], xqs[c][:, g, cols], "wx", g) for g in range(KP)]
                steps += [(hq[a, c][:, cols], hqs[a, c][:, cols], "wh", a) for a in range(2)]
                for dst, todo in ((pt, steps), (st, [(hq[a, c][:, cols], hqs[a, c][:, cols], "v1", a) for a in range(2)])):
                    for k, (q, qs, n, g) in enumerate(todo):
                        nc.tensor.matmul_mx(out=dst[:, i, :], lhsT=q.bitcast(X4), lhsT_scale=qs,
                                            rhs=small[n][0][:, g, :].bitcast(X4), rhs_scale=small[n][1][:, g, :],
                                            start=(k == 0), stop=(k == len(todo) - 1))
            pp[c] = pt
            ps[c] = st

        def tanh(c):
            e = epool.tile([P, RT, C], F32, tag="e")
            nc.scalar.activation(out=e[:], in_=pp[c][:], func=ACT.Tanh)
            sc[c] = e

        def score(c):
            yc = y2[:, RT * c:RT * c + RT, :]
            nc.vector.tensor_tensor(out=sc[c][:], in0=ps[c][:], in1=sc[c][:], op=ALU.add)
            nc.vector.tensor_tensor(out=sc[c][:], in0=sc[c][:], in1=yc, op=ALU.mult)

        def expo(c):
            nc.scalar.activation(out=sc[c][:], in_=sc[c][:], func=ACT.Exp, scale=-1.6, bias=LN2)

        def target(c):
            yc = y2[:, RT * c:RT * c + RT, :]
            o = epool.tile([P, RT, C], F32, tag="o")
            nc.vector.scalar_tensor_tensor(out=o[:], in0=sc[c][:], scalar=2.0, in1=yc, op0=ALU.add, op1=ALU.mult)
            nc.sync.dma_start(out=out_view[:, RT * c:RT * c + RT, :], in_=o[:])

        for s in range(CH + 2):
            if s < CH:
                for t in range(4):
                    if (t, s) not in done:
                        centre(1, s, t, flat=(s >= 5))
            if 2 <= s:
                score(s - 2)
                expo(s - 2)
            if s < CH:
                words(1, s)
            if 1 <= s <= CH:
                quant_h(1, s - 1)
                stage2(s - 1)
                tanh(s - 1)
            if 2 <= s:
                target(s - 2)
